import numpy as np
import ml_dtypes


def mxq(x, axis, fmt="e4m3"):
    dtype, down = {"e4m3": (ml_dtypes.float8_e4m3fn, 7), "e5m2": (ml_dtypes.float8_e5m2, 14)}[fmt]
    v = np.moveaxis(np.asarray(x, np.float32).astype(ml_dtypes.bfloat16).astype(np.float64), axis, -1)
    blocks = v.reshape(v.shape[:-1] + (-1, 32))
    amax = np.abs(blocks).max(-1, keepdims=True)
    byte = np.maximum(np.where(amax > 0, np.frexp(amax)[1] - 1 + 127, 0) - down, 1)
    scale = np.exp2(byte - 127.0)
    codes = (blocks / scale).astype(np.float32).astype(dtype).astype(np.float64)
    return np.moveaxis((codes * scale).reshape(v.shape), -1, axis)


WIDE = False


def mx_kscale(k):
    if not WIDE:
        return np.ones(k)
    levels = np.array([10, -10, 5, -5, 0])
    if k % 512:
        return np.exp2(np.random.permutation(np.resize(levels, k // 32))).repeat(32)
    a = np.empty((k // 512, 16))
    for p in range(k // 512):
        a[p, :8] = np.random.permutation(np.resize(levels, 8))
        for g in range(8):
            far = levels[np.abs(levels - a[p, g]) >= 10]
            a[p, g + 8] = far[np.random.randint(len(far))]
    return np.exp2(a.ravel()).repeat(32)


def f64(x):
    return np.asarray(x).astype(np.float64)


def striped(idx):
    return np.tile(np.asarray(idx).reshape(-1, 16).T, (8, 1)).astype(np.uint16)


def unstriped(offs):
    return offs[:16].T.reshape(-1).astype(np.int64)


E2M1 = np.array([0.0, 0.5, 1.0, 1.5, 2.0, 3.0, 4.0, 6.0, -0.0, -0.5, -1.0, -1.5, -2.0, -3.0, -4.0, -6.0])


def pack_weight(w, fmt):
    k, n = w.shape
    w = f64(np.asarray(w, np.float32).astype(ml_dtypes.bfloat16)).reshape(k // 32, 32, n)
    amax = np.abs(w).max(1)
    if fmt == "e4m3":
        byte = np.frexp(amax)[1] - 1 + 127 - 7
    else:
        mant, ex = np.frexp(amax / 6.0)
        byte = np.where(mant > 0.5, ex, ex - 1) + 127
    byte = np.clip(np.where(amax > 0, byte, 1), 1, 254)
    scaled = (w * np.exp2(127.0 - byte)[:, None, :]).reshape(k, n).astype(np.float32)
    by_word = np.ascontiguousarray(scaled.reshape(k // 512, 128, 4, n).transpose(0, 1, 3, 2))
    if fmt == "e4m3":
        words = by_word.astype(ml_dtypes.float8_e4m3fn).view(np.uint8)
    else:
        c = by_word.astype(ml_dtypes.float4_e2m1fn).view(np.uint8) & 0xF
        words = (c[..., 0::2] | (c[..., 1::2] << 4)).reshape(k // 512, 128, 2 * n)
    return np.ascontiguousarray(words), np.ascontiguousarray(byte.astype(np.uint8).reshape(k // 512, 16, n))


def unpack_weight(words, scales, fmt):
    g, _, n = scales.shape
    words = np.ascontiguousarray(words).reshape(g, 128, n, -1)
    if fmt == "e4m3":
        vals = words.view(ml_dtypes.float8_e4m3fn).astype(np.float64)
    else:
        nib = np.empty((g, 128, n, 4), np.uint8)
        nib[..., 0::2] = words & 0xF
        nib[..., 1::2] = words >> 4
        vals = E2M1[nib]
    vals = vals * np.repeat(np.exp2(scales.astype(np.float64) - 127.0), 8, axis=1)[..., None]
    return vals.transpose(0, 1, 3, 2).reshape(g * 512, n)


D, E, T, I, Q = 512, 512, 2048, 512, 128


def setup_inputs():
    n = np.random.standard_normal
    idx = np.random.permutation(T)[:I]
    fd = mx_kscale(D)
    fe = mx_kscale(E)
    fi = mx_kscale(I)
    ti = np.ones(T)
    ti[idx] = fi
    keysp = pack_weight(n((D, T)) / fd[:, None], "e4m3")
    valsp = pack_weight(n((E, T)) / fe[:, None], "e4m3")
    return {
        "query": (n((D, Q)) * 0.8 / np.sqrt(D) * fd[:, None]).astype(np.float32),
        "keys_words": keysp[0],
        "keys_scales": keysp[1],
        "bonus": (np.random.uniform(0.5, 2.0, (Q, 1))).astype(np.float32),
        "gout": (n((E, Q)) * 1 / np.sqrt(E) * fe[:, None]).astype(np.float32),
        "vals_words": valsp[0],
        "vals_scales": valsp[1],
        "fs": (np.random.uniform(128.0, 512.0, (1, I)) * fi).astype(np.float32),
        "keyrows": (n((D, T)) / ti).astype(np.float32),
        "res": (n((Q, D)) * 4.0).astype(np.float32),
        "offs": striped(idx),
    }


def reference(query, keys_words, keys_scales, bonus, gout, vals_words, vals_scales, fs, keyrows, res, offs):
    idx = unstriped(offs)
    keysu = unpack_weight(keys_words, keys_scales, "e4m3")
    valsu = unpack_weight(vals_words, vals_scales, "e4m3")
    queryq = mxq(f64(query), 0, "e4m3")
    keysidxg = keysu[:, idx]
    a = queryq.T @ keysidxg
    b = a - np.max(a, axis=1, keepdims=True)
    p = np.exp(b)
    z = np.sum(p, axis=1, keepdims=True)
    goutq = mxq(f64(gout), 0, "e4m3")
    valsidxg = valsu[:, idx]
    c0 = goutq.T @ valsidxg
    dz = f64(bonus) / z - np.sum(p * c0, axis=1, keepdims=True) / np.square(z) - f64(bonus) * (-1.0) * np.sum(p * b, axis=1, keepdims=True) / np.square(z)
    dp = 1.0 / z * c0 + f64(bonus) * (-1.0) / z * b + dz
    db = f64(bonus) * (-1.0) / z * p + dp * p
    gs = db * f64(fs)
    gt1 = gs.T
    kt = f64(keyrows)[:, idx].T
    gt1q = mxq(gt1, 0, "e4m3")
    ktq = mxq(kt, 0, "e4m3")
    gq = gt1q.T @ ktq
    y = gq + f64(res)
    return y

@@ -1,0 +1,177 @@
+from contextlib import ExitStack
+
+import concourse.mybir as mybir
+from concourse.masks import make_identity
+
+F32 = mybir.dt.float32
+BF16 = mybir.dt.bfloat16
+I32 = mybir.dt.int32
+U32 = mybir.dt.uint32
+U16 = mybir.dt.uint16
+U8 = mybir.dt.uint8
+FP8X4 = mybir.dt.float8_e4m3fn_x4
+ALU = mybir.AluOpType
+ACT = mybir.ActivationFunctionType
+AXIS = mybir.AxisListType
+
+P = 128
+PACK = 4
+TOKENS = 2048
+SLOTS = 512
+ROWS = 128
+FEATURES = 512
+PLANES = FEATURES // P
+QUADRANTS = 4
+VALS_SCALE_ROW = 4
+
+FLOPS = 3 * 2 * ROWS * SLOTS * FEATURES
+
+
+def tile_attend_bentropybonus_q_kernel(
+    tc, query, keys_words, keys_scales, bonus, gout, vals_words, vals_scales, fs, keyrows, res, offs, out
+):
+    nc = tc.nc
+    with ExitStack() as ctx:
+        held = ctx.enter_context(tc.tile_pool(name="held", bufs=1))
+        windows = ctx.enter_context(tc.tile_pool(name="windows", bufs=1))
+        banks = ctx.enter_context(tc.psum_pool(name="banks", bufs=1))
+        turn_banks = ctx.enter_context(tc.psum_pool(name="turn_banks", bufs=2))
+        out_banks = ctx.enter_context(tc.psum_pool(name="out_banks", bufs=3))
+
+        offsets = held.tile([P, SLOTS // 16], U16, name="offsets")
+        nc.sync.dma_start(offsets[:], offs)
+
+        def load_scales(name, slot, scales, first_row, queue):
+            window = windows.tile([P, TOKENS], U8, name=name, tag=slot, align_bytes=64)
+            nc.vector.memset(window[:].bitcast(I32), 0)
+            for quad in range(QUADRANTS):
+                row = 32 * quad + first_row
+                queue.dma_start(
+                    window[row : row + 4, :].bitcast(I32), scales[0, 4 * quad : 4 * quad + 4, :].bitcast(I32)
+                )
+            return window
+
+        def load_words(name, slot, words):
+            window = windows.tile([P, TOKENS], I32, name=name, tag=slot, align_bytes=64)
+            nc.sync.dma_start(window[:], words[0].rearrange("p n t -> p (n t)").bitcast(I32))
+            return window
+
+        def load_rows(name, slot, source):
+            raw = windows.tile([P, PACK, ROWS], F32, name=name, tag=slot, align_bytes=64)
+            nc.sync.dma_start(raw[:], source.rearrange("(p j) w -> p j w", j=PACK))
+            return raw
+
+        def quantize(name, grouped, width):
+            codes = held.tile([P, width], U32, name=name + "_codes", align_bytes=64)
+            scales = held.tile([P, width], U8, name=name + "_scales", align_bytes=64)
+            nc.vector.quantize_mx(out=codes[:].bitcast(FP8X4), scales=scales[:], in_=grouped)
+            return codes, scales
+
+        def quantize_rows(name, slot, raw):
+            grouped = windows.tile([P, ROWS, PACK], BF16, name=name + "_grouped", tag=slot, align_bytes=64)
+            nc.scalar.copy(out=grouped[:], in_=raw[:].rearrange("p j w -> p w j"))
+            return quantize(name, grouped[:].rearrange("p w j -> p (w j)"), ROWS)
+
+        def gather(name, slot, window, dtype):
+            picked = windows.tile([P, SLOTS], dtype, name=name, tag=slot, align_bytes=64)
+            nc.vector.tensor_copy(picked[:], window.indirect(offsets[:]))
+            return picked
+
+        bonus_col = held.tile([P, 1], F32, name="bonus_col")
+        nc.sync.dma_start(bonus_col[:], bonus)
+        query_raw = load_rows("query_raw", "slot2", query)
+        gout_raw = load_rows("gout_raw", "slot4", gout)
+        keys_word_window = load_words("keys_word_window", "slot0", keys_words)
+        keys_scale_window = load_scales("keys_scale_window", "slot5", keys_scales, 0, nc.scalar)
+        vals_scale_window = load_scales("vals_scale_window", "slot6", vals_scales, VALS_SCALE_ROW, nc.gpsimd)
+        identity = held.tile([P, P], F32, name="identity")
+        make_identity(nc, identity[:])
+
+        query_codes, query_scale = quantize_rows("query", "slot1", query_raw)
+        vals_word_window = load_words("vals_word_window", "slot2", vals_words)
+        gout_codes, gout_scale = quantize_rows("gout", "slot8", gout_raw)
+        fs_cols = windows.tile([P, PACK], F32, name="fs_cols", tag="slot4", align_bytes=64)
+        nc.sync.dma_start(fs_cols[:], fs.rearrange("o (p t) -> (o p) t", t=PACK))
+        keys_scale = gather("keys_scale", "slot1", keys_scale_window[:], U8)
+        keys_codes = gather("keys_codes", "slot5", keys_word_window[:].bitcast(U32), U32)
+        score = banks.tile([P, SLOTS], F32, name="score")
+        nc.tensor.matmul_mx(
+            out=score[:], lhsT=query_codes[:].bitcast(FP8X4), lhsT_scale=query_scale[:],
+            rhs=keys_codes[:].bitcast(FP8X4), rhs_scale=keys_scale[:], start=True, stop=True,
+        )
+        vals_scale = gather("vals_scale", "slot7", vals_scale_window[:], U8)
+        neg_max = held.tile([P, 1], F32, name="neg_max")
+        nc.vector.tensor_reduce(neg_max[:], score[:], AXIS.X, ALU.max, negate=True)
+        weight = held.tile([P, SLOTS], F32, name="weight")
+        weight_sum = held.tile([P, 1], F32, name="weight_sum")
+        nc.scalar.activation(weight[:], score[:], ACT.Exp, bias=neg_max[:], accum_out=weight_sum[:])
+        bonus_score = windows.tile([P, SLOTS], F32, name="bonus_score", tag="slot3", align_bytes=64)
+        nc.scalar.activation(bonus_score[:], score[:], ACT.Copy, scale=bonus_col[:])
+
+        vals_codes = gather("vals_codes", "slot6", vals_word_window[:].bitcast(U32), U32)
+        read_grad = banks.tile([P, SLOTS], F32, name="read_grad")
+        nc.tensor.matmul_mx(
+            out=read_grad[:], lhsT=gout_codes[:].bitcast(FP8X4), lhsT_scale=gout_scale[:],
+            rhs=vals_codes[:].bitcast(FP8X4), rhs_scale=vals_scale[VALS_SCALE_ROW:P, :], start=True, stop=True,
+        )
+        inv_sum = held.tile([P, 1], F32, name="inv_sum")
+        nc.vector.reciprocal(inv_sum[:], weight_sum[:])
+        prob = held.tile([P, SLOTS], F32, name="prob", tag="prob", align_bytes=64)
+        nc.scalar.activation(prob[:], weight[:], ACT.Copy, scale=inv_sum[:])
+
+        def turn_plane(plane, slot):
+            window = windows.tile([P, TOKENS], F32, name="keyrows_window%d" % plane, tag="slot%d" % plane, align_bytes=64)
+            nc.sync.dma_start(window[:], keyrows[plane * P : (plane + 1) * P, :])
+            picked = held.tile([P, SLOTS], BF16, name="picked%d" % plane, tag=slot, align_bytes=64)
+            nc.vector.tensor_copy(picked[:], window[:].indirect(offsets[:]))
+            pairs = picked[:].bitcast(F32)
+            turned = turn_banks.tile([P, 2, P], F32, name="turned")
+            for half in range(2):
+                nc.tensor.transpose(turned[:, half, :], pairs[:, half : SLOTS // 2 : 2], identity[:])
+            grouped = held.tile([P, P, PACK], BF16, name="keyrows_grouped%d" % plane, tag="grouped%d" % plane, align_bytes=64)
+            nc.scalar.copy(
+                out=grouped[:].rearrange("p d t -> p (d t)").bitcast(F32).rearrange("p (d u) -> p d u", u=2),
+                in_=turned[:].rearrange("p u d -> p d u"),
+            )
+            return grouped
+
+        def quantize_plane(plane, slot):
+            grouped = turn_plane(plane, slot)
+            return quantize("keyrows%d" % plane, grouped[:].rearrange("p d t -> p (d t)"), P)
+
+        neg_slope = held.tile([P, SLOTS], F32, name="neg_slope", tag="slope", align_bytes=64)
+        nc.vector.tensor_tensor(neg_slope[:], bonus_score[:], read_grad[:], ALU.subtract)
+        neg_product = held.tile([P, SLOTS], F32, name="neg_product", tag="product", align_bytes=64)
+        neg_mean = held.tile([P, 1], F32, name="neg_mean")
+        nc.vector.scalar_tensor_tensor(
+            neg_product[:], neg_slope[:], 1.0, prob[:], ALU.mult, ALU.mult, accum_out=neg_mean[:]
+        )
+        planes = [quantize_plane(0, "slope")]
+        score_grad = held.tile([P, SLOTS], F32, name="score_grad", tag="late")
+        nc.vector.scalar_tensor_tensor(score_grad[:], prob[:], neg_mean[:], neg_product[:], ALU.mult, ALU.subtract)
+        grad_turned = banks.tile([P, PACK, ROWS], F32, name="grad_turned")
+        grad_grouped = held.tile([P, ROWS, PACK], BF16, name="grad_grouped", tag="grad_grouped", align_bytes=64)
+        for place in range(PACK):
+            nc.tensor.transpose(grad_turned[:, place, :], score_grad[:, place:SLOTS:PACK], identity[:])
+        for place in range(PACK):
+            nc.scalar.activation(
+                grad_grouped[:, :, place], grad_turned[:, place, :], ACT.Copy, scale=fs_cols[:, place : place + 1]
+            )
+
+        planes.extend([quantize_plane(1, "prob"), quantize_plane(2, "product")])
+        grad_codes, grad_scale = quantize("grad", grad_grouped[:].rearrange("p q t -> p (q t)"), ROWS)
+        planes.append(quantize_plane(3, "grad_grouped"))
+
+        residual = held.tile([P, FEATURES], F32, name="residual", tag="late")
+        nc.sync.dma_start(residual[:], res)
+
+        for plane, (codes, scale) in enumerate(planes):
+            total = out_banks.tile([P, P], F32, name="total")
+            nc.tensor.matmul_mx(
+                out=total[:], lhsT=grad_codes[:].bitcast(FP8X4), lhsT_scale=grad_scale[:],
+                rhs=codes[:].bitcast(FP8X4), rhs_scale=scale[:], start=True, stop=True,
+            )
+            result = held.tile([P, P], F32, name="result%d" % plane)
+            cols = slice(plane * P, (plane + 1) * P)
+            nc.vector.tensor_tensor(result[:], total[:], residual[:, cols], ALU.add)
+            nc.sync.dma_start(out[:, cols], result[:])

@@ -1,7 +1,6 @@
 from contextlib import ExitStack
 
 import concourse.mybir as mybir
-from concourse.masks import make_identity
 
 F32 = mybir.dt.float32
 BF16 = mybir.dt.bfloat16
@@ -24,6 +23,17 @@ PLANES = FEATURES // P
 QUADRANTS = 4
 VALS_SCALE_ROW = 4
 
+KEYS_AT = 0
+QUERY_SCALE_AT = KEYS_AT + 4 * TOKENS
+GOUT_SCALE_AT = QUERY_SCALE_AT + ROWS
+VALS_SCALE_AT = GOUT_SCALE_AT + ROWS
+ONES_AT = QUERY_SCALE_AT - 128
+KEYS_SCALE_AT = VALS_SCALE_AT + TOKENS
+BONUS_AT = KEYS_SCALE_AT + SLOTS
+QUERY_GROUPED_AT = BONUS_AT - 64
+FS_AT = BONUS_AT + 64
+VALS_AT = FS_AT + 64
+
 FLOPS = 3 * 2 * ROWS * SLOTS * FEATURES
 
 
@@ -34,93 +44,110 @@ def tile_attend_bentropybonus_q_kernel(
     with ExitStack() as ctx:
         held = ctx.enter_context(tc.tile_pool(name="held", bufs=1))
         windows = ctx.enter_context(tc.tile_pool(name="windows", bufs=1))
+        placed = ctx.enter_context(tc.tile_pool(name="placed", bufs=1))
         banks = ctx.enter_context(tc.psum_pool(name="banks", bufs=1))
         turn_banks = ctx.enter_context(tc.psum_pool(name="turn_banks", bufs=2))
-        out_banks = ctx.enter_context(tc.psum_pool(name="out_banks", bufs=3))
+        out_banks = ctx.enter_context(tc.psum_pool(name="out_banks", bufs=1))
 
         offsets = held.tile([P, SLOTS // 16], U16, name="offsets")
         nc.sync.dma_start(offsets[:], offs)
 
-        def load_scales(name, slot, scales, first_row, queue):
-            window = windows.tile([P, TOKENS], U8, name=name, tag=slot, align_bytes=64)
+        def load_scales(window, scales, first_row):
             nc.vector.memset(window[:].bitcast(I32), 0)
             for quad in range(QUADRANTS):
                 row = 32 * quad + first_row
-                queue.dma_start(
+                nc.sync.dma_start(
                     window[row : row + 4, :].bitcast(I32), scales[0, 4 * quad : 4 * quad + 4, :].bitcast(I32)
                 )
-            return window
 
-        def load_words(name, slot, words):
-            window = windows.tile([P, TOKENS], I32, name=name, tag=slot, align_bytes=64)
+        def load_words(name, at, words):
+            window = placed.tile([P, TOKENS], I32, name=name, offset=at)
             nc.sync.dma_start(window[:], words[0].rearrange("p n t -> p (n t)").bitcast(I32))
             return window
 
-        def load_rows(name, slot, source):
-            raw = windows.tile([P, PACK, ROWS], F32, name=name, tag=slot, align_bytes=64)
+        def load_rows(raw, source):
             nc.sync.dma_start(raw[:], source.rearrange("(p j) w -> p j w", j=PACK))
-            return raw
 
-        def quantize(name, grouped, width):
-            codes = held.tile([P, width], U32, name=name + "_codes", align_bytes=64)
-            scales = held.tile([P, width], U8, name=name + "_scales", align_bytes=64)
-            nc.vector.quantize_mx(out=codes[:].bitcast(FP8X4), scales=scales[:], in_=grouped)
-            return codes, scales
+        def quantize(codes, grouped, scales):
+            nc.vector.quantize_mx(
+                out=codes[:].bitcast(FP8X4), scales=scales[:], in_=grouped[:].rearrange("p w j -> p (w j)")
+            )
 
-        def quantize_rows(name, slot, raw):
-            grouped = windows.tile([P, ROWS, PACK], BF16, name=name + "_grouped", tag=slot, align_bytes=64)
+        def interleave(grouped, raw):
             nc.scalar.copy(out=grouped[:], in_=raw[:].rearrange("p j w -> p w j"))
-            return quantize(name, grouped[:].rearrange("p w j -> p (w j)"), ROWS)
 
-        def gather(name, slot, window, dtype):
-            picked = windows.tile([P, SLOTS], dtype, name=name, tag=slot, align_bytes=64)
+        def gather(picked, window):
             nc.vector.tensor_copy(picked[:], window.indirect(offsets[:]))
-            return picked
 
-        bonus_col = held.tile([P, 1], F32, name="bonus_col")
-        nc.sync.dma_start(bonus_col[:], bonus)
-        query_raw = load_rows("query_raw", "slot2", query)
-        gout_raw = load_rows("gout_raw", "slot4", gout)
-        keys_word_window = load_words("keys_word_window", "slot0", keys_words)
-        keys_scale_window = load_scales("keys_scale_window", "slot5", keys_scales, 0, nc.scalar)
-        vals_scale_window = load_scales("vals_scale_window", "slot6", vals_scales, VALS_SCALE_ROW, nc.gpsimd)
+        query_raw = held.tile([P, PACK, ROWS], F32, name="query_raw")
+        load_rows(query_raw, query)
+        gout_raw = held.tile([P, PACK, ROWS], F32, name="gout_raw")
+        load_rows(gout_raw, gout)
+        keys_scale_window = windows.tile([P, TOKENS], U8, name="keys_scale_window", tag="slot3", align_bytes=64)
+        load_scales(keys_scale_window, keys_scales, 0)
+        ones = placed.tile([P, P], F32, name="ones", offset=ONES_AT)
+        nc.gpsimd.memset(ones[:], 1.0)
         identity = held.tile([P, P], F32, name="identity")
-        make_identity(nc, identity[:])
+        nc.gpsimd.affine_select(
+            out=identity[:], in_=ones[:], pattern=[[-1, P]], compare_op=ALU.is_equal, fill=0.0,
+            base=0, channel_multiplier=1,
+        )
+        keys_word_window = load_words("keys_word_window", KEYS_AT, keys_words)
+        vals_scale_window = placed.tile([P, TOKENS], U8, name="vals_scale_window", offset=VALS_SCALE_AT)
+        load_scales(vals_scale_window, vals_scales, VALS_SCALE_ROW)
 
-        query_codes, query_scale = quantize_rows("query", "slot1", query_raw)
-        vals_word_window = load_words("vals_word_window", "slot2", vals_words)
-        gout_codes, gout_scale = quantize_rows("gout", "slot8", gout_raw)
-        fs_cols = windows.tile([P, PACK], F32, name="fs_cols", tag="slot4", align_bytes=64)
+        query_grouped = placed.tile([P, ROWS, PACK], BF16, name="query_grouped", offset=QUERY_GROUPED_AT, align_bytes=64)
+        interleave(query_grouped, query_raw)
+        query_scale = placed.tile([P, ROWS], U8, name="query_scale", offset=QUERY_SCALE_AT, align_bytes=64)
+        query_codes = windows.tile([P, ROWS], U32, name="query_codes", tag="slot1", align_bytes=64)
+        quantize(query_codes, query_grouped, query_scale)
+        vals_word_window = load_words("vals_word_window", VALS_AT, vals_words)
+        bonus_col = placed.tile([P, 1], F32, name="bonus_col", offset=BONUS_AT)
+        nc.sync.dma_start(bonus_col[:], bonus)
+        fs_cols = placed.tile([P, PACK], F32, name="fs_cols", offset=FS_AT)
         nc.sync.dma_start(fs_cols[:], fs.rearrange("o (p t) -> (o p) t", t=PACK))
-        keys_scale = gather("keys_scale", "slot1", keys_scale_window[:], U8)
-        keys_codes = gather("keys_codes", "slot5", keys_word_window[:].bitcast(U32), U32)
+        keys_scale = placed.tile([P, SLOTS], U8, name="keys_scale", offset=KEYS_SCALE_AT, align_bytes=64)
+        gather(keys_scale, keys_scale_window[:])
+        gout_grouped = windows.tile([P, ROWS, PACK], BF16, name="gout_grouped", tag="slot0", align_bytes=64)
+        interleave(gout_grouped, gout_raw)
+        gout_scale = placed.tile([P, ROWS], U8, name="gout_scale", offset=GOUT_SCALE_AT, align_bytes=64)
+        gout_codes = held.tile([P, ROWS], U32, name="gout_codes", align_bytes=64)
+        quantize(gout_codes, gout_grouped, gout_scale)
+        keys_codes = windows.tile([P, SLOTS], U32, name="keys_codes", tag="slot3", align_bytes=64)
+        gather(keys_codes, keys_word_window[:].bitcast(U32))
         score = banks.tile([P, SLOTS], F32, name="score")
         nc.tensor.matmul_mx(
             out=score[:], lhsT=query_codes[:].bitcast(FP8X4), lhsT_scale=query_scale[:],
             rhs=keys_codes[:].bitcast(FP8X4), rhs_scale=keys_scale[:], start=True, stop=True,
         )
-        vals_scale = gather("vals_scale", "slot7", vals_scale_window[:], U8)
-        neg_max = held.tile([P, 1], F32, name="neg_max")
+        vals_scale = placed.tile([P, SLOTS], U8, name="vals_scale", offset=KEYS_AT, align_bytes=64)
+        gather(vals_scale, vals_scale_window[:])
+        neg_max = windows.tile([P, 1], F32, name="neg_max", tag="slot2", align_bytes=64)
         nc.vector.tensor_reduce(neg_max[:], score[:], AXIS.X, ALU.max, negate=True)
         weight = held.tile([P, SLOTS], F32, name="weight")
         weight_sum = held.tile([P, 1], F32, name="weight_sum")
         nc.scalar.activation(weight[:], score[:], ACT.Exp, bias=neg_max[:], accum_out=weight_sum[:])
-        bonus_score = windows.tile([P, SLOTS], F32, name="bonus_score", tag="slot3", align_bytes=64)
+        bonus_score = held.tile([P, SLOTS], F32, name="bonus_score", tag="late")
         nc.scalar.activation(bonus_score[:], score[:], ACT.Copy, scale=bonus_col[:])
 
-        vals_codes = gather("vals_codes", "slot6", vals_word_window[:].bitcast(U32), U32)
+        vals_codes = windows.tile([P, SLOTS], U32, name="vals_codes", tag="slot3", align_bytes=64)
+        gather(vals_codes, vals_word_window[:].bitcast(U32))
         read_grad = banks.tile([P, SLOTS], F32, name="read_grad")
         nc.tensor.matmul_mx(
             out=read_grad[:], lhsT=gout_codes[:].bitcast(FP8X4), lhsT_scale=gout_scale[:],
             rhs=vals_codes[:].bitcast(FP8X4), rhs_scale=vals_scale[VALS_SCALE_ROW:P, :], start=True, stop=True,
         )
-        inv_sum = held.tile([P, 1], F32, name="inv_sum")
+        inv_sum = placed.tile([P, 1], F32, name="inv_sum", offset=VALS_AT)
         nc.vector.reciprocal(inv_sum[:], weight_sum[:])
         prob = held.tile([P, SLOTS], F32, name="prob", tag="prob", align_bytes=64)
         nc.scalar.activation(prob[:], weight[:], ACT.Copy, scale=inv_sum[:])
 
         def turn_plane(plane, slot):
-            window = windows.tile([P, TOKENS], F32, name="keyrows_window%d" % plane, tag="slot%d" % plane, align_bytes=64)
+            name = "keyrows_window%d" % plane
+            if plane < PLANES - 1:
+                window = windows.tile([P, TOKENS], F32, name=name, tag="slot%d" % plane, align_bytes=64)
+            else:
+                window = placed.tile([P, TOKENS], F32, name=name, offset=KEYS_AT)
             nc.sync.dma_start(window[:], keyrows[plane * P : (plane + 1) * P, :])
             picked = held.tile([P, SLOTS], BF16, name="picked%d" % plane, tag=slot, align_bytes=64)
             nc.vector.tensor_copy(picked[:], window[:].indirect(offsets[:]))
@@ -135,10 +162,6 @@ def tile_attend_bentropybonus_q_kernel(
             )
             return grouped
 
-        def quantize_plane(plane, slot):
-            grouped = turn_plane(plane, slot)
-            return quantize("keyrows%d" % plane, grouped[:].rearrange("p d t -> p (d t)"), P)
-
         neg_slope = held.tile([P, SLOTS], F32, name="neg_slope", tag="slope", align_bytes=64)
         nc.vector.tensor_tensor(neg_slope[:], bonus_score[:], read_grad[:], ALU.subtract)
         neg_product = held.tile([P, SLOTS], F32, name="neg_product", tag="product", align_bytes=64)
@@ -146,8 +169,8 @@ def tile_attend_bentropybonus_q_kernel(
         nc.vector.scalar_tensor_tensor(
             neg_product[:], neg_slope[:], 1.0, prob[:], ALU.mult, ALU.mult, accum_out=neg_mean[:]
         )
-        planes = [quantize_plane(0, "slope")]
-        score_grad = held.tile([P, SLOTS], F32, name="score_grad", tag="late")
+        grouped_planes = [turn_plane(0, "slope")]
+        score_grad = held.tile([P, SLOTS], F32, name="score_grad")
         nc.vector.scalar_tensor_tensor(score_grad[:], prob[:], neg_mean[:], neg_product[:], ALU.mult, ALU.subtract)
         grad_turned = banks.tile([P, PACK, ROWS], F32, name="grad_turned")
         grad_grouped = held.tile([P, ROWS, PACK], BF16, name="grad_grouped", tag="grad_grouped", align_bytes=64)
@@ -158,20 +181,39 @@ def tile_attend_bentropybonus_q_kernel(
                 grad_grouped[:, :, place], grad_turned[:, place, :], ACT.Copy, scale=fs_cols[:, place : place + 1]
             )
 
-        planes.extend([quantize_plane(1, "prob"), quantize_plane(2, "product")])
-        grad_codes, grad_scale = quantize("grad", grad_grouped[:].rearrange("p q t -> p (q t)"), ROWS)
-        planes.append(quantize_plane(3, "grad_grouped"))
+        grouped_planes.append(turn_plane(1, "prob"))
+
+        def quantize_plane(plane, codes):
+            scale = held.tile([P, P], U8, name="keyrows_scale%d" % plane, align_bytes=64)
+            quantize(codes, grouped_planes[plane], scale)
+            return codes, scale
+
+        def late_codes(name, place):
+            return placed.tile([P, P], U32, name=name, offset=KEYS_AT + 4 * P * place, align_bytes=64)
+
+        planes = [quantize_plane(0, windows.tile([P, P], U32, name="keyrows_codes0", tag="slot1", align_bytes=64))]
+        grouped_planes.append(turn_plane(2, "product"))
+        grouped_planes.append(turn_plane(3, "slope"))
+        grad_scale = held.tile([P, ROWS], U8, name="grad_scale", align_bytes=64)
+        grad_codes = late_codes("grad_codes", 0)
+        quantize(grad_codes, grad_grouped, grad_scale)
+        for plane in range(1, PLANES):
+            planes.append(quantize_plane(plane, late_codes("keyrows_codes%d" % plane, plane)))
 
         residual = held.tile([P, FEATURES], F32, name="residual", tag="late")
         nc.sync.dma_start(residual[:], res)
 
-        for plane, (codes, scale) in enumerate(planes):
-            total = out_banks.tile([P, P], F32, name="total")
-            nc.tensor.matmul_mx(
-                out=total[:], lhsT=grad_codes[:].bitcast(FP8X4), lhsT_scale=grad_scale[:],
-                rhs=codes[:].bitcast(FP8X4), rhs_scale=scale[:], start=True, stop=True,
-            )
-            result = held.tile([P, P], F32, name="result%d" % plane)
-            cols = slice(plane * P, (plane + 1) * P)
+        for first, last in ((0, PLANES - 1), (PLANES - 1, PLANES)):
+            width = (last - first) * P
+            total = out_banks.tile([P, width], F32, name="total%d" % first)
+            for plane in range(first, last):
+                codes, scale = planes[plane]
+                nc.tensor.matmul_mx(
+                    out=total[:, (plane - first) * P : (plane - first + 1) * P],
+                    lhsT=grad_codes[:].bitcast(FP8X4), lhsT_scale=grad_scale[:],
+                    rhs=codes[:].bitcast(FP8X4), rhs_scale=scale[:], start=True, stop=True,
+                )
+            result = held.tile([P, width], F32, name="result%d" % first)
+            cols = slice(first * P, last * P)
             nc.vector.tensor_tensor(result[:], total[:], residual[:, cols], ALU.add)
             nc.sync.dma_start(out[:, cols], result[:])

@@ -46,7 +46,7 @@ def tile_attend_bentropybonus_q_kernel(
         windows = ctx.enter_context(tc.tile_pool(name="windows", bufs=1))
         placed = ctx.enter_context(tc.tile_pool(name="placed", bufs=1))
         banks = ctx.enter_context(tc.psum_pool(name="banks", bufs=1))
-        turn_banks = ctx.enter_context(tc.psum_pool(name="turn_banks", bufs=2))
+        turn_banks = ctx.enter_context(tc.psum_pool(name="turn_banks", bufs=3))
         out_banks = ctx.enter_context(tc.psum_pool(name="out_banks", bufs=1))
 
         offsets = held.tile([P, SLOTS // 16], U16, name="offsets")
@@ -101,11 +101,11 @@ def tile_attend_bentropybonus_q_kernel(
         query_scale = placed.tile([P, ROWS], U8, name="query_scale", offset=QUERY_SCALE_AT, align_bytes=64)
         query_codes = windows.tile([P, ROWS], U32, name="query_codes", tag="slot1", align_bytes=64)
         quantize(query_codes, query_grouped, query_scale)
-        vals_word_window = load_words("vals_word_window", VALS_AT, vals_words)
         bonus_col = placed.tile([P, 1], F32, name="bonus_col", offset=BONUS_AT)
         nc.sync.dma_start(bonus_col[:], bonus)
         fs_cols = placed.tile([P, PACK], F32, name="fs_cols", offset=FS_AT)
         nc.sync.dma_start(fs_cols[:], fs.rearrange("o (p t) -> (o p) t", t=PACK))
+        vals_word_window = load_words("vals_word_window", VALS_AT, vals_words)
         keys_scale = placed.tile([P, SLOTS], U8, name="keys_scale", offset=KEYS_SCALE_AT, align_bytes=64)
         gather(keys_scale, keys_scale_window[:])
         gout_grouped = windows.tile([P, ROWS, PACK], BF16, name="gout_grouped", tag="slot0", align_bytes=64)
@@ -125,7 +125,7 @@ def tile_attend_bentropybonus_q_kernel(
         neg_max = windows.tile([P, 1], F32, name="neg_max", tag="slot2", align_bytes=64)
         nc.vector.tensor_reduce(neg_max[:], score[:], AXIS.X, ALU.max, negate=True)
         weight = held.tile([P, SLOTS], F32, name="weight")
-        weight_sum = held.tile([P, 1], F32, name="weight_sum")
+        weight_sum = held.tile([P, 1], F32, name="weight_sum", tag="weight_sum", align_bytes=64)
         nc.scalar.activation(weight[:], score[:], ACT.Exp, bias=neg_max[:], accum_out=weight_sum[:])
         bonus_score = held.tile([P, SLOTS], F32, name="bonus_score", tag="late")
         nc.scalar.activation(bonus_score[:], score[:], ACT.Copy, scale=bonus_col[:])
@@ -142,78 +142,80 @@ def tile_attend_bentropybonus_q_kernel(
         prob = held.tile([P, SLOTS], F32, name="prob", tag="prob", align_bytes=64)
         nc.scalar.activation(prob[:], weight[:], ACT.Copy, scale=inv_sum[:])
 
-        def turn_plane(plane, slot):
+        def turn_plane(plane, picked, grouped):
             name = "keyrows_window%d" % plane
             if plane < PLANES - 1:
                 window = windows.tile([P, TOKENS], F32, name=name, tag="slot%d" % plane, align_bytes=64)
             else:
                 window = placed.tile([P, TOKENS], F32, name=name, offset=KEYS_AT)
             nc.sync.dma_start(window[:], keyrows[plane * P : (plane + 1) * P, :])
-            picked = held.tile([P, SLOTS], BF16, name="picked%d" % plane, tag=slot, align_bytes=64)
-            nc.vector.tensor_copy(picked[:], window[:].indirect(offsets[:]))
+            gather(picked, window[:])
             pairs = picked[:].bitcast(F32)
             turned = turn_banks.tile([P, 2, P], F32, name="turned")
             for half in range(2):
                 nc.tensor.transpose(turned[:, half, :], pairs[:, half : SLOTS // 2 : 2], identity[:])
-            grouped = held.tile([P, P, PACK], BF16, name="keyrows_grouped%d" % plane, tag="grouped%d" % plane, align_bytes=64)
             nc.scalar.copy(
-                out=grouped[:].rearrange("p d t -> p (d t)").bitcast(F32).rearrange("p (d u) -> p d u", u=2),
+                out=grouped.rearrange("p d t -> p (d t)").bitcast(F32).rearrange("p (d u) -> p d u", u=2),
                 in_=turned[:].rearrange("p u d -> p d u"),
             )
-            return grouped
 
-        neg_slope = held.tile([P, SLOTS], F32, name="neg_slope", tag="slope", align_bytes=64)
+        def picked_tile(plane, pool, slot):
+            return pool.tile([P, SLOTS], BF16, name="picked%d" % plane, tag=slot, align_bytes=64)
+
+        grouped_pair = held.tile([P, 2 * P, PACK], BF16, name="grouped_pair", align_bytes=64)
+        grouped_third = held.tile([P, P, PACK], BF16, name="grouped_third", align_bytes=64)
+        grouped_last = held.tile([P, P, PACK], BF16, name="grouped_last", tag="last", align_bytes=64)
+
+        turn_plane(0, picked_tile(0, held, "weight_sum"), grouped_pair[:, 0:P, :])
+        neg_slope = windows.tile([P, SLOTS], F32, name="neg_slope", tag="slot0", align_bytes=64)
         nc.vector.tensor_tensor(neg_slope[:], bonus_score[:], read_grad[:], ALU.subtract)
         neg_product = held.tile([P, SLOTS], F32, name="neg_product", tag="product", align_bytes=64)
         neg_mean = held.tile([P, 1], F32, name="neg_mean")
         nc.vector.scalar_tensor_tensor(
             neg_product[:], neg_slope[:], 1.0, prob[:], ALU.mult, ALU.mult, accum_out=neg_mean[:]
         )
-        grouped_planes = [turn_plane(0, "slope")]
+        residual = held.tile([P, FEATURES], F32, name="residual", tag="late")
+        nc.sync.dma_start(residual[:], res)
         score_grad = held.tile([P, SLOTS], F32, name="score_grad")
         nc.vector.scalar_tensor_tensor(score_grad[:], prob[:], neg_mean[:], neg_product[:], ALU.mult, ALU.subtract)
         grad_turned = banks.tile([P, PACK, ROWS], F32, name="grad_turned")
-        grad_grouped = held.tile([P, ROWS, PACK], BF16, name="grad_grouped", tag="grad_grouped", align_bytes=64)
+        grad_grouped = held.tile([P, ROWS, PACK], BF16, name="grad_grouped", align_bytes=64)
         for place in range(PACK):
             nc.tensor.transpose(grad_turned[:, place, :], score_grad[:, place:SLOTS:PACK], identity[:])
         for place in range(PACK):
             nc.scalar.activation(
                 grad_grouped[:, :, place], grad_turned[:, place, :], ACT.Copy, scale=fs_cols[:, place : place + 1]
             )
+        turn_plane(1, picked_tile(1, held, "prob"), grouped_pair[:, P : 2 * P, :])
+        turn_plane(2, picked_tile(2, held, "product"), grouped_third[:])
+        turn_plane(3, picked_tile(3, windows, "slot0"), grouped_last[:])
 
-        grouped_planes.append(turn_plane(1, "prob"))
-
-        def quantize_plane(plane, codes):
-            scale = held.tile([P, P], U8, name="keyrows_scale%d" % plane, align_bytes=64)
-            quantize(codes, grouped_planes[plane], scale)
+        def quantize_late(name, grouped, first_word, width):
+            codes = placed.tile([P, width], U32, name=name + "_codes", offset=KEYS_AT + 4 * first_word, align_bytes=64)
+            scale = held.tile([P, width], U8, name=name + "_scale", align_bytes=64)
+            quantize(codes, grouped, scale)
             return codes, scale
 
-        def late_codes(name, place):
-            return placed.tile([P, P], U32, name=name, offset=KEYS_AT + 4 * P * place, align_bytes=64)
+        grad_codes, grad_scale = quantize_late("grad", grad_grouped, FEATURES, ROWS)
+        pair = quantize_late("pair", grouped_pair, 0, 2 * P)
+        third = quantize_late("third", grouped_third, 2 * P, P)
+        last = quantize_late("last", grouped_last, 3 * P, P)
 
-        planes = [quantize_plane(0, windows.tile([P, P], U32, name="keyrows_codes0", tag="slot1", align_bytes=64))]
-        grouped_planes.append(turn_plane(2, "product"))
-        grouped_planes.append(turn_plane(3, "slope"))
-        grad_scale = held.tile([P, ROWS], U8, name="grad_scale", align_bytes=64)
-        grad_codes = late_codes("grad_codes", 0)
-        quantize(grad_codes, grad_grouped, grad_scale)
-        for plane in range(1, PLANES):
-            planes.append(quantize_plane(plane, late_codes("keyrows_codes%d" % plane, plane)))
-
-        residual = held.tile([P, FEATURES], F32, name="residual", tag="late")
-        nc.sync.dma_start(residual[:], res)
-
-        for first, last in ((0, PLANES - 1), (PLANES - 1, PLANES)):
-            width = (last - first) * P
-            total = out_banks.tile([P, width], F32, name="total%d" % first)
-            for plane in range(first, last):
-                codes, scale = planes[plane]
+        def finish(name, parts, first, slot):
+            width = sum(codes.shape[1] for codes, scale in parts)
+            total = out_banks.tile([P, width], F32, name=name + "_total")
+            at = 0
+            for codes, scale in parts:
                 nc.tensor.matmul_mx(
-                    out=total[:, (plane - first) * P : (plane - first + 1) * P],
+                    out=total[:, at : at + codes.shape[1]],
                     lhsT=grad_codes[:].bitcast(FP8X4), lhsT_scale=grad_scale[:],
                     rhs=codes[:].bitcast(FP8X4), rhs_scale=scale[:], start=True, stop=True,
                 )
-            result = held.tile([P, width], F32, name="result%d" % first)
-            cols = slice(first * P, last * P)
+                at = at + codes.shape[1]
+            result = held.tile([P, width], F32, name=name + "_result", tag=slot, align_bytes=64)
+            cols = slice(first, first + width)
             nc.vector.tensor_tensor(result[:], total[:], residual[:, cols], ALU.add)
             nc.sync.dma_start(out[:, cols], result[:])
+
+        finish("front", [pair, third], 0, "last")
+        finish("back", [last], 3 * P, "back")

@@ -101,11 +101,11 @@ def tile_attend_bentropybonus_q_kernel(
         query_scale = placed.tile([P, ROWS], U8, name="query_scale", offset=QUERY_SCALE_AT, align_bytes=64)
         query_codes = windows.tile([P, ROWS], U32, name="query_codes", tag="slot1", align_bytes=64)
         quantize(query_codes, query_grouped, query_scale)
+        vals_word_window = load_words("vals_word_window", VALS_AT, vals_words)
         bonus_col = placed.tile([P, 1], F32, name="bonus_col", offset=BONUS_AT)
         nc.sync.dma_start(bonus_col[:], bonus)
         fs_cols = placed.tile([P, PACK], F32, name="fs_cols", offset=FS_AT)
         nc.sync.dma_start(fs_cols[:], fs.rearrange("o (p t) -> (o p) t", t=PACK))
-        vals_word_window = load_words("vals_word_window", VALS_AT, vals_words)
         keys_scale = placed.tile([P, SLOTS], U8, name="keys_scale", offset=KEYS_SCALE_AT, align_bytes=64)
         gather(keys_scale, keys_scale_window[:])
         gout_grouped = windows.tile([P, ROWS, PACK], BF16, name="gout_grouped", tag="slot0", align_bytes=64)

from contextlib import ExitStack

import concourse.mybir as mybir

F32 = mybir.dt.float32
BF16 = mybir.dt.bfloat16
I32 = mybir.dt.int32
U32 = mybir.dt.uint32
U16 = mybir.dt.uint16
U8 = mybir.dt.uint8
FP8X4 = mybir.dt.float8_e4m3fn_x4
ALU = mybir.AluOpType
ACT = mybir.ActivationFunctionType
AXIS = mybir.AxisListType

P = 128
PACK = 4
TOKENS = 2048
SLOTS = 512
ROWS = 128
FEATURES = 512
PLANES = FEATURES // P
QUADRANTS = 4
VALS_SCALE_ROW = 4

KEYS_AT = 0
QUERY_SCALE_AT = KEYS_AT + 4 * TOKENS
GOUT_SCALE_AT = QUERY_SCALE_AT + ROWS
VALS_SCALE_AT = GOUT_SCALE_AT + ROWS
ONES_AT = QUERY_SCALE_AT - 128
KEYS_SCALE_AT = VALS_SCALE_AT + TOKENS
BONUS_AT = KEYS_SCALE_AT + SLOTS
QUERY_GROUPED_AT = BONUS_AT - 64
FS_AT = BONUS_AT + 64
VALS_AT = FS_AT + 64

FLOPS = 3 * 2 * ROWS * SLOTS * FEATURES


def tile_attend_bentropybonus_q_kernel(
    tc, query, keys_words, keys_scales, bonus, gout, vals_words, vals_scales, fs, keyrows, res, offs, out
):
    nc = tc.nc
    with ExitStack() as ctx:
        held = ctx.enter_context(tc.tile_pool(name="held", bufs=1))
        windows = ctx.enter_context(tc.tile_pool(name="windows", bufs=1))
        placed = ctx.enter_context(tc.tile_pool(name="placed", bufs=1))
        banks = ctx.enter_context(tc.psum_pool(name="banks", bufs=1))
        turn_banks = ctx.enter_context(tc.psum_pool(name="turn_banks", bufs=3))
        out_banks = ctx.enter_context(tc.psum_pool(name="out_banks", bufs=1))

        offsets = held.tile([P, SLOTS // 16], U16, name="offsets")
        nc.sync.dma_start(offsets[:], offs)

        def load_scales(window, scales, first_row):
            nc.vector.memset(window[:].bitcast(I32), 0)
            for quad in range(QUADRANTS):
                row = 32 * quad + first_row
                nc.sync.dma_start(
                    window[row : row + 4, :].bitcast(I32), scales[0, 4 * quad : 4 * quad + 4, :].bitcast(I32)
                )

        def load_words(name, at, words):
            window = placed.tile([P, TOKENS], I32, name=name, offset=at)
            nc.sync.dma_start(window[:], words[0].rearrange("p n t -> p (n t)").bitcast(I32))
            return window

        def load_rows(raw, source):
            nc.sync.dma_start(raw[:], source.rearrange("(p j) w -> p j w", j=PACK))

        def quantize(codes, grouped, scales):
            nc.vector.quantize_mx(
                out=codes[:].bitcast(FP8X4), scales=scales[:], in_=grouped[:].rearrange("p w j -> p (w j)")
            )

        def interleave(grouped, raw):
            nc.scalar.copy(out=grouped[:], in_=raw[:].rearrange("p j w -> p w j"))

        def gather(picked, window):
            nc.vector.tensor_copy(picked[:], window.indirect(offsets[:]))

        query_raw = held.tile([P, PACK, ROWS], F32, name="query_raw")
        load_rows(query_raw, query)
        gout_raw = held.tile([P, PACK, ROWS], F32, name="gout_raw")
        load_rows(gout_raw, gout)
        keys_scale_window = windows.tile([P, TOKENS], U8, name="keys_scale_window", tag="slot3", align_bytes=64)
        load_scales(keys_scale_window, keys_scales, 0)
        ones = placed.tile([P, P], F32, name="ones", offset=ONES_AT)
        nc.gpsimd.memset(ones[:], 1.0)
        identity = held.tile([P, P], F32, name="identity")
        nc.gpsimd.affine_select(
            out=identity[:], in_=ones[:], pattern=[[-1, P]], compare_op=ALU.is_equal, fill=0.0,
            base=0, channel_multiplier=1,
        )
        keys_word_window = load_words("keys_word_window", KEYS_AT, keys_words)
        vals_scale_window = placed.tile([P, TOKENS], U8, name="vals_scale_window", offset=VALS_SCALE_AT)
        load_scales(vals_scale_window, vals_scales, VALS_SCALE_ROW)

        query_grouped = placed.tile([P, ROWS, PACK], BF16, name="query_grouped", offset=QUERY_GROUPED_AT, align_bytes=64)
        interleave(query_grouped, query_raw)
        query_scale = placed.tile([P, ROWS], U8, name="query_scale", offset=QUERY_SCALE_AT, align_bytes=64)
        query_codes = windows.tile([P, ROWS], U32, name="query_codes", tag="slot1", align_bytes=64)
        quantize(query_codes, query_grouped, query_scale)
        vals_word_window = load_words("vals_word_window", VALS_AT, vals_words)
        bonus_col = placed.tile([P, 1], F32, name="bonus_col", offset=BONUS_AT)
        nc.sync.dma_start(bonus_col[:], bonus)
        fs_cols = placed.tile([P, PACK], F32, name="fs_cols", offset=FS_AT)
        nc.sync.dma_start(fs_cols[:], fs.rearrange("o (p t) -> (o p) t", t=PACK))
        keys_scale = placed.tile([P, SLOTS], U8, name="keys_scale", offset=KEYS_SCALE_AT, align_bytes=64)
        gather(keys_scale, keys_scale_window[:])
        gout_grouped = windows.tile([P, ROWS, PACK], BF16, name="gout_grouped", tag="slot0", align_bytes=64)
        interleave(gout_grouped, gout_raw)
        gout_scale = placed.tile([P, ROWS], U8, name="gout_scale", offset=GOUT_SCALE_AT, align_bytes=64)
        gout_codes = held.tile([P, ROWS], U32, name="gout_codes", align_bytes=64)
        quantize(gout_codes, gout_grouped, gout_scale)
        keys_codes = windows.tile([P, SLOTS], U32, name="keys_codes", tag="slot3", align_bytes=64)
        gather(keys_codes, keys_word_window[:].bitcast(U32))
        score = banks.tile([P, SLOTS], F32, name="score")
        nc.tensor.matmul_mx(
            out=score[:], lhsT=query_codes[:].bitcast(FP8X4), lhsT_scale=query_scale[:],
            rhs=keys_codes[:].bitcast(FP8X4), rhs_scale=keys_scale[:], start=True, stop=True,
        )
        vals_scale = placed.tile([P, SLOTS], U8, name="vals_scale", offset=KEYS_AT, align_bytes=64)
        gather(vals_scale, vals_scale_window[:])
        neg_max = windows.tile([P, 1], F32, name="neg_max", tag="slot2", align_bytes=64)
        nc.vector.tensor_reduce(neg_max[:], score[:], AXIS.X, ALU.max, negate=True)
        weight = held.tile([P, SLOTS], F32, name="weight")
        weight_sum = held.tile([P, 1], F32, name="weight_sum", tag="weight_sum", align_bytes=64)
        nc.scalar.activation(weight[:], score[:], ACT.Exp, bias=neg_max[:], accum_out=weight_sum[:])
        bonus_score = held.tile([P, SLOTS], F32, name="bonus_score", tag="late")
        nc.scalar.activation(bonus_score[:], score[:], ACT.Copy, scale=bonus_col[:])

        vals_codes = windows.tile([P, SLOTS], U32, name="vals_codes", tag="slot3", align_bytes=64)
        gather(vals_codes, vals_word_window[:].bitcast(U32))
        read_grad = banks.tile([P, SLOTS], F32, name="read_grad")
        nc.tensor.matmul_mx(
            out=read_grad[:], lhsT=gout_codes[:].bitcast(FP8X4), lhsT_scale=gout_scale[:],
            rhs=vals_codes[:].bitcast(FP8X4), rhs_scale=vals_scale[VALS_SCALE_ROW:P, :], start=True, stop=True,
        )
        inv_sum = placed.tile([P, 1], F32, name="inv_sum", offset=VALS_AT)
        nc.vector.reciprocal(inv_sum[:], weight_sum[:])
        prob = held.tile([P, SLOTS], F32, name="prob", tag="prob", align_bytes=64)
        nc.scalar.activation(prob[:], weight[:], ACT.Copy, scale=inv_sum[:])

        def turn_plane(plane, picked, grouped):
            name = "keyrows_window%d" % plane
            if plane < PLANES - 1:
                window = windows.tile([P, TOKENS], F32, name=name, tag="slot%d" % plane, align_bytes=64)
            else:
                window = placed.tile([P, TOKENS], F32, name=name, offset=KEYS_AT)
            nc.sync.dma_start(window[:], keyrows[plane * P : (plane + 1) * P, :])
            gather(picked, window[:])
            pairs = picked[:].bitcast(F32)
            turned = turn_banks.tile([P, 2, P], F32, name="turned")
            for half in range(2):
                nc.tensor.transpose(turned[:, half, :], pairs[:, half : SLOTS // 2 : 2], identity[:])
            nc.scalar.copy(
                out=grouped.rearrange("p d t -> p (d t)").bitcast(F32).rearrange("p (d u) -> p d u", u=2),
                in_=turned[:].rearrange("p u d -> p d u"),
            )

        def picked_tile(plane, pool, slot):
            return pool.tile([P, SLOTS], BF16, name="picked%d" % plane, tag=slot, align_bytes=64)

        grouped_pair = held.tile([P, 2 * P, PACK], BF16, name="grouped_pair", align_bytes=64)
        grouped_third = held.tile([P, P, PACK], BF16, name="grouped_third", align_bytes=64)
        grouped_last = held.tile([P, P, PACK], BF16, name="grouped_last", tag="last", align_bytes=64)

        turn_plane(0, picked_tile(0, held, "weight_sum"), grouped_pair[:, 0:P, :])
        neg_slope = windows.tile([P, SLOTS], F32, name="neg_slope", tag="slot0", align_bytes=64)
        nc.vector.tensor_tensor(neg_slope[:], bonus_score[:], read_grad[:], ALU.subtract)
        neg_product = held.tile([P, SLOTS], F32, name="neg_product", tag="product", align_bytes=64)
        neg_mean = held.tile([P, 1], F32, name="neg_mean")
        nc.vector.scalar_tensor_tensor(
            neg_product[:], neg_slope[:], 1.0, prob[:], ALU.mult, ALU.mult, accum_out=neg_mean[:]
        )
        residual = held.tile([P, FEATURES], F32, name="residual", tag="late")
        nc.sync.dma_start(residual[:], res)
        score_grad = held.tile([P, SLOTS], F32, name="score_grad")
        nc.vector.scalar_tensor_tensor(score_grad[:], prob[:], neg_mean[:], neg_product[:], ALU.mult, ALU.subtract)
        grad_turned = banks.tile([P, PACK, ROWS], F32, name="grad_turned")
        grad_grouped = held.tile([P, ROWS, PACK], BF16, name="grad_grouped", align_bytes=64)
        for place in range(PACK):
            nc.tensor.transpose(grad_turned[:, place, :], score_grad[:, place:SLOTS:PACK], identity[:])
        for place in range(PACK):
            nc.scalar.activation(
                grad_grouped[:, :, place], grad_turned[:, place, :], ACT.Copy, scale=fs_cols[:, place : place + 1]
            )
        turn_plane(1, picked_tile(1, held, "prob"), grouped_pair[:, P : 2 * P, :])
        turn_plane(2, picked_tile(2, held, "product"), grouped_third[:])
        turn_plane(3, picked_tile(3, windows, "slot0"), grouped_last[:])

        def quantize_late(name, grouped, first_word, width):
            codes = placed.tile([P, width], U32, name=name + "_codes", offset=KEYS_AT + 4 * first_word, align_bytes=64)
            scale = held.tile([P, width], U8, name=name + "_scale", align_bytes=64)
            quantize(codes, grouped, scale)
            return codes, scale

        grad_codes, grad_scale = quantize_late("grad", grad_grouped, FEATURES, ROWS)
        pair = quantize_late("pair", grouped_pair, 0, 2 * P)
        third = quantize_late("third", grouped_third, 2 * P, P)
        last = quantize_late("last", grouped_last, 3 * P, P)

        def finish(name, parts, first, slot):
            width = sum(codes.shape[1] for codes, scale in parts)
            total = out_banks.tile([P, width], F32, name=name + "_total")
            at = 0
            for codes, scale in parts:
                nc.tensor.matmul_mx(
                    out=total[:, at : at + codes.shape[1]],
                    lhsT=grad_codes[:].bitcast(FP8X4), lhsT_scale=grad_scale[:],
                    rhs=codes[:].bitcast(FP8X4), rhs_scale=scale[:], start=True, stop=True,
                )
                at = at + codes.shape[1]
            result = held.tile([P, width], F32, name=name + "_result", tag=slot, align_bytes=64)
            cols = slice(first, first + width)
            nc.vector.tensor_tensor(result[:], total[:], residual[:, cols], ALU.add)
            nc.sync.dma_start(out[:, cols], result[:])

        finish("front", [pair, third], 0, "last")
        finish("back", [last], 3 * P, "back")
